import numpy as np, ml_dtypes
CORES = [3,7,11,15,131,135,139,143]
N = 8
import mx_ref
NC = 128
C2 = np.float32(0.344)
BF = ml_dtypes.bfloat16
def cut(t, i, w=512):
    return t[:, w * i:w * i + w]
def tile(rs):
    return np.stack(rs, axis=2).reshape(128, -1).astype(BF)
def pick(b):
    s = np.zeros((128, 128, 4), np.float32)
    s[np.arange(128), np.arange(128), b] = 1.0
    return mx_ref.quantize(s.reshape(128, 512).astype(BF))
def setup_inputs(rng):
    def f(*shape):
        return mx_ref.flush((rng.standard_normal(shape, dtype=np.float32) * np.exp2(rng.integers(-2, 3, shape[:-1] + (1,)))).astype(BF))
    return {"b": f(N, 128, N * 512), "x": f(N, 128, 4 * NC)}
def setup_inputs_blocks(rng):
    d = setup_inputs(rng)
    for k in ("b", "x"): d[k] = mx_ref.spread(d[k], rng, 2)
    return d
def setup_inputs_wide(rng):
    d = setup_inputs(rng)
    for k in ("b", "x"): d[k] = mx_ref.flush((d[k].astype(np.float32) * np.exp2(rng.integers(-4, 5, (N, 1, 1))).astype(np.float32)).astype(BF))
    return d
def reference(b, x, own=None):
    S = [pick(t) for t in range(4)]
    h = np.zeros((N, 128, 512), BF)
    for c in range(N):
        for r in range(N):
            q = mx_ref.quantize(cut(b[r], c))
            P = [mx_ref.matmul(S[t], q) for t in range(4)]
            Z = P if r == 0 else [z + p for z, p in zip(Z, P)]
        h[c] = tile([np.maximum(Z[t], 0) * C2 for t in range(4)])
    use = h if own is None else own["h"]
    H = [mx_ref.quantize(use[j]) for j in range(N)]
    y = np.zeros((N, 128, N * NC), np.float32)
    for r in range(N):
        qx = mx_ref.quantize(x[r])
        for j in range(N):
            y[r][:, NC * j:NC * j + NC] = mx_ref.matmul(H[j], qx)
    return {"h": h, "y": y}

@@ -1,0 +1,233 @@
+import numpy as np
+from concourse.bass import DstId, RemoteDMATransfer
+from concourse.mybir import dt, AluOpType, ActivationFunctionType
+
+N = 8
+W = 128
+E = 4 * W
+BANK = 512
+C2 = float(np.float32(0.344))
+
+SLOTS = [("plane", True), ("far", True), ("plane", False), ("far", False), ("mate", True), ("mate", False), ("peer", False)]
+
+SCRATCH = {
+    "bt": ("sbuf", [128, N * E], "bfloat16"),
+    "q": ("sbuf", [128, N * W], "float8_e4m3fn_x4"),
+    "qs": ("sbuf", [128, N * W], "uint8"),
+    "land": ("sbuf", [128, N * W], "float8_e4m3fn_x4"),
+    "lands": ("sbuf", [128, N * W], "uint8"),
+    "xt": ("sbuf", [128, E], "bfloat16"),
+    "xq": ("sbuf", [128, W], "float8_e4m3fn_x4"),
+    "xs": ("sbuf", [128, W], "uint8"),
+    "ones": ("sbuf", [128, W], "bfloat16"),
+    "diag": ("sbuf", [128, E + 4], "bfloat16"),
+    "sq": ("sbuf", [128, 4 * W], "float8_e4m3fn_x4"),
+    "ss": ("sbuf", [128, 4 * W], "uint8"),
+    "ht": ("sbuf", [128, E], "bfloat16"),
+    "hq": ("sbuf", [128, W], "float8_e4m3fn_x4"),
+    "hs": ("sbuf", [128, W], "uint8"),
+    "hl": ("sbuf", [128, 7 * W], "float8_e4m3fn_x4"),
+    "hls": ("sbuf", [128, 7 * W], "uint8"),
+    "yt": ("sbuf", [128, N * W], "float32"),
+    "ps": ("psum", [128, 8 * BANK], "float32"),
+}
+SEMAPHORES = (["fill", "dia", "sdone", "xload", "xdone", "hop", "hdone", "sent1", "sent2", "sent3", "stored",
+               "hpeer", "hcod", "hsca", "hfwd", "hmate"]
+              + ["bload%d" % i for i in range(4)] + ["bdone%d" % i for i in range(4)]
+              + ["from%d" % i for i in range(N)] + ["z%d" % i for i in range(4)]
+              + ["yps%d" % i for i in range(N)] + ["ysb%d" % i for i in range(N)])
+
+
+def _engines(mask):
+    return [i for i in range(mask.bit_length()) if mask >> i & 1]
+
+
+def _split(mask, k):
+    e = _engines(mask)
+    n = len(e) // k
+    return [sum(1 << i for i in e[j * n:j * n + n]) for j in range(k)]
+
+
+def _place(topo, a, b):
+    if (topo.host(a), topo.chip(a)) == (topo.host(b), topo.chip(b)):
+        kind = "own" if a == b else "peer"
+    elif topo.mates(a, b):
+        kind = "mate"
+    elif topo.same_plane(a, b):
+        kind = "plane"
+    else:
+        kind = "far"
+    return kind, topo.die(a) == topo.die(b)
+
+
+def rank_program(g, core, T, topo):
+    me = T.rank_of(core)
+    if me is None:
+        return
+    cores = list(T.cores)
+    rank = {_place(topo, core, c): r for r, c in enumerate(cores)}
+    chip_of = {k: sorted(r for (kind, same), r in rank.items() if (kind == k or (k == "own" and kind == "peer")))
+               for k in ("far", "mate", "plane", "own")}
+    order = ["far", "mate", "plane", "own"]
+    peer = cores[rank["peer", False]]
+    off = topo.mask(core, cores[rank["far", True]])
+    inner = topo.mask(core, peer) & ~off
+    sem = T.sem
+    cnt = lambda m: len(_engines(m))
+
+    def tile(buf, i, n=1):
+        return buf[:, W * i:W * (i + n)]
+
+    def bytes_(ap):
+        return ap.bitcast(dt.uint8)
+
+    def send(mask, rsem, src, dests):
+        ids = []
+        for c, _ in dests:
+            rid, pid = topo.addr(c, core)
+            ids.append(DstId(rid=rid, pnc=pid))
+        return RemoteDMATransfer(dst_ids=ids, dma_engine_mask=mask, remote_sem=rsem, srcs=[src], dsts=[v for _, v in dests])
+
+    for i, k in enumerate(order):
+        lo, hi = E * chip_of[k][0], E * (chip_of[k][-1] + 1)
+        g.sync.dma_start(T.bt[0:64, lo:hi], T.b[0:64, lo:hi]).then_inc(sem["bload%d" % i], 16)
+        g.scalar.dma_start(T.bt[64:128, lo:hi], T.b[64:128, lo:hi]).then_inc(sem["bload%d" % i], 16)
+
+    g.vector.memset(T.ones[:], 1.0).then_inc(sem.fill, 1)
+    g.vector.memset(T.diag[:], 0.0).then_inc(sem.fill, 1)
+    g.wait_ge(sem.fill, 2)
+    g.affine_select(T.diag[:, 3:3 + E:4], T.ones[:], [[1, W]], AluOpType.is_equal, 0.0, 0, -1).then_inc(sem.dia, 1)
+    g.vector.wait_ge(sem.dia, 1)
+    for b in range(4):
+        g.vector.quantize_mx(tile(T.sq, b), tile(T.ss, b), T.diag[:, 3 - b:3 - b + E]).then_inc(sem.sdone, 1)
+
+    for i, k in enumerate(order):
+        r0, n = chip_of[k][0], len(chip_of[k])
+        g.vector.wait_ge(sem["bload%d" % i], 32)
+        g.vector.quantize_mx(tile(T.q, r0, n), tile(T.qs, r0, n),
+                             T.bt[:, E * r0:E * (r0 + n)]).then_inc(sem["bdone%d" % i], 1)
+
+    def scatter(plan):
+        mine = sem["from%d" % me]
+        g.remote_dma_fused([send(m, mine, bytes_(tile(T.q, r)), [(cores[r], bytes_(tile(T.land, me)))])
+                            for r, m in plan], local_sem=sem.sent1)
+        g.remote_dma_fused([send(m, mine, tile(T.qs, r), [(cores[r], tile(T.lands, me))])
+                            for r, m in plan], local_sem=sem.sent1)
+        return 2 * sum(cnt(m) for _, m in plan)
+
+    plan1 = list(zip(chip_of["far"], _split(off, 2)))
+    plan2 = list(zip(chip_of["mate"] + chip_of["plane"], _split(off, 4))) + [(rank["peer", False], inner)]
+    g.wait_ge(sem.bdone0, 1)
+    out1 = scatter(plan1)
+    for i in (1, 2, 3):
+        g.wait_ge(sem["bdone%d" % i], 1)
+    out1 += scatter(plan2)
+    came = {}
+    for r, m in plan1 + plan2:
+        came[r] = 2 * cnt(m)
+
+    g.tensor.wait_ge(sem.sdone, 4)
+    g.tensor.wait_ge(sem.bdone3, 1)
+    sources = [me] + [rank[p] for p in (("far", True), ("far", False), ("peer", False), ("mate", True), ("mate", False),
+                                        ("plane", True), ("plane", False))]
+    for i, r in enumerate(sources):
+        cod, sca = (T.q, T.qs) if r == me else (T.land, T.lands)
+        if r != me:
+            g.tensor.wait_ge(sem["from%d" % r], came[r])
+        for b in range(4):
+            mm = g.tensor.matmul_mx(T.ps[:, BANK * b:BANK * b + W], tile(T.sq, b), tile(T.ss, b),
+                                    tile(cod, r), tile(sca, r), i == 0, i == N - 1)
+            if i == N - 1:
+                mm.then_inc(sem["z%d" % b], 1)
+
+    for b in (0, 2):
+        g.scalar.wait_ge(sem["z%d" % b], 1)
+        g.scalar.activation(T.ht[:, b:E:4], T.ps[:, BANK * b:BANK * b + W], ActivationFunctionType.Relu,
+                            scale=C2).then_inc(sem.hop, 1)
+    for b in (1, 3):
+        g.vector.wait_ge(sem["z%d" % b], 1)
+        g.vector.tensor_scalar(T.ht[:, b:E:4], T.ps[:, BANK * b:BANK * b + W], 0.0, C2,
+                               AluOpType.max, AluOpType.mult).then_inc(sem.hop, 1)
+    g.vector.wait_ge(sem.hop, 4)
+    g.vector.quantize_mx(T.hq[:], T.hs[:], T.ht[:]).then_inc(sem.hdone, 1)
+
+    g.sync.wait_ge(sem.sent1, out1)
+    g.sync.dma_start(T.xt[:], T.x[:]).then_inc(sem.xload, 16)
+    g.vector.wait_ge(sem.xload, 16)
+    g.vector.quantize_mx(T.xq[:], T.xs[:], T.xt[:]).then_inc(sem.xdone, 1)
+
+    slot = {p: i for i, p in enumerate(SLOTS)}
+
+    def there(buf, p):
+        return cores[rank[p]], tile(buf, slot[p])
+
+    def there8(p):
+        c, v = there(T.hl, p)
+        return c, bytes_(v)
+
+    first = [("plane", True), ("far", True)]
+    near = ("peer", False)
+    mate = [("mate", True), ("mate", False)]
+    g.wait_ge(sem.hdone, 1)
+    g.remote_dma_fused([send(off, sem.hcod, bytes_(T.hq[:]), [there8(p) for p in first]),
+                        send(inner, sem.hpeer, bytes_(T.hq[:]), [there8(near)])], local_sem=sem.sent2)
+    g.remote_dma_fused([send(off, sem.hsca, T.hs[:], [there(T.hls, p) for p in first]),
+                        send(inner, sem.hpeer, T.hs[:], [there(T.hls, near)])], local_sem=sem.sent2)
+    g.remote_dma_fused([send(off, sem.hmate, bytes_(T.hq[:]), [there8(p) for p in mate])], local_sem=sem.sent2)
+    g.remote_dma_fused([send(off, sem.hmate, T.hs[:], [there(T.hls, p) for p in mate])], local_sem=sem.sent2)
+    out2 = 4 * cnt(off) + 2 * cnt(inner)
+    rid, pid = topo.addr(peer, core)
+    s0, o0 = slot["plane", True], slot["plane", False]
+    g.wait_ge(sem.hcod, 2 * cnt(off))
+    g.remote_dma(bytes_(tile(T.hl, o0, 2)), bytes_(tile(T.hl, s0, 2)), sem.hfwd, sem.sent3, pid, rid, inner)
+    g.wait_ge(sem.hsca, 2 * cnt(off))
+    g.remote_dma(tile(T.hls, o0, 2), tile(T.hls, s0, 2), sem.hfwd, sem.sent3, pid, rid, inner)
+    g.wait_ge(sem.sent3, 2 * cnt(inner))
+
+    arrive = {"own": [], "peer": [("hpeer", 2 * cnt(inner))], "mate": [("hmate", 4 * cnt(off))],
+              True: [("hcod", 2 * cnt(off)), ("hsca", 2 * cnt(off))], False: [("hfwd", 2 * cnt(inner))]}
+    blocks = [("own", True), near, ("plane", True), ("far", True), ("mate", True), ("mate", False),
+              ("plane", False), ("far", False)]
+    g.tensor.wait_ge(sem.hdone, 1)
+    g.tensor.wait_ge(sem.xdone, 1)
+    for i, p in enumerate(blocks):
+        j = rank[p]
+        bank = BANK * ((i + 4) % 8)
+        if p[0] == "own":
+            w, ws = T.hq[:], T.hs[:]
+        else:
+            for s, v in arrive[p[0] if p[0] in arrive else p[1]]:
+                g.tensor.wait_ge(sem[s], v)
+            w, ws = tile(T.hl, slot[p]), tile(T.hls, slot[p])
+        g.tensor.matmul_mx(T.ps[:, bank:bank + W], w, ws, T.xq[:], T.xs[:], True, True).then_inc(sem["yps%d" % j], 1)
+    stores = [0]
+
+    def store(queue, js):
+        for j in js:
+            queue.wait_ge(sem["ysb%d" % j], 1)
+        lo, hi = W * js[0], W * (js[-1] + 1)
+        queue.dma_start(T.y[:, lo:hi], T.yt[:, lo:hi]).then_inc(sem.stored, 16)
+        stores[0] += 1
+
+    for i, p in enumerate(blocks):
+        j = rank[p]
+        bank = BANK * ((i + 4) % 8)
+        if i % 2 == 0:
+            g.vector.wait_ge(sem["yps%d" % j], 1)
+            g.vector.tensor_copy(tile(T.yt, j), T.ps[:, bank:bank + W]).then_inc(sem["ysb%d" % j], 1)
+        else:
+            g.scalar.wait_ge(sem["yps%d" % j], 1)
+            g.scalar.activation(tile(T.yt, j), T.ps[:, bank:bank + W],
+                                ActivationFunctionType.Copy).then_inc(sem["ysb%d" % j], 1)
+        if p == ("mate", False):
+            store(g.scalar, chip_of["mate"])
+    store(g.scalar, [rank["far", False]])
+
+    g.sync.wait_ge(sem.sent2, out2)
+    store(g.sync, chip_of["own"])
+    store(g.sync, [rank["plane", True]])
+    store(g.sync, [rank["far", True]])
+    g.sync.wait_ge(sem.hop, 4)
+    g.sync.dma_start(T.h[:], T.ht[:]).then_inc(sem.stored, 16)
+    store(g.sync, [rank["plane", False]])
+    g.sync.wait_ge(sem.stored, 16 * (stores[0] + 1))

@@ -8,7 +8,15 @@ E = 4 * W
 BANK = 512
 C2 = float(np.float32(0.344))
 
-SLOTS = [("plane", True), ("far", True), ("plane", False), ("far", False), ("mate", True), ("mate", False), ("peer", False)]
+OWN, PEER = ("own", True), ("peer", False)
+MATE, MATE_X = ("mate", True), ("mate", False)
+PLANE, PLANE_X = ("plane", True), ("plane", False)
+FAR, FAR_X = ("far", True), ("far", False)
+
+LOADS = [[PLANE], [FAR, FAR_X], [PLANE_X], [MATE, MATE_X], [OWN, PEER]]
+SUMS = [OWN, PLANE, FAR, FAR_X, PEER, MATE, PLANE_X, MATE_X]
+SLOTS = [PLANE, FAR, PLANE_X, FAR_X, MATE, MATE_X, PEER]
+BLOCKS = [OWN, PEER, PLANE, FAR, MATE, MATE_X, PLANE_X, FAR_X]
 
 SCRATCH = {
     "bt": ("sbuf", [128, N * E], "bfloat16"),
@@ -32,8 +40,8 @@ SCRATCH = {
     "ps": ("psum", [128, 8 * BANK], "float32"),
 }
 SEMAPHORES = (["fill", "dia", "sdone", "xload", "xdone", "hop", "hdone", "sent1", "sent2", "sent3", "stored",
-               "hpeer", "hcod", "hsca", "hfwd", "hmate"]
-              + ["bload%d" % i for i in range(4)] + ["bdone%d" % i for i in range(4)]
+               "hpeer", "hplane", "hfar", "hmate", "hmatex", "hsca", "hfwd"]
+              + ["bload%d" % i for i in range(len(LOADS))] + ["bdone%d" % i for i in range(len(LOADS))]
               + ["from%d" % i for i in range(N)] + ["z%d" % i for i in range(4)]
               + ["yps%d" % i for i in range(N)] + ["ysb%d" % i for i in range(N)])
 
@@ -61,17 +69,16 @@ def _place(topo, a, b):
 
 
 def rank_program(g, core, T, topo):
+    cores = list(T.cores)
     me = T.rank_of(core)
     if me is None:
         return
-    cores = list(T.cores)
     rank = {_place(topo, core, c): r for r, c in enumerate(cores)}
-    chip_of = {k: sorted(r for (kind, same), r in rank.items() if (kind == k or (k == "own" and kind == "peer")))
-               for k in ("far", "mate", "plane", "own")}
-    order = ["far", "mate", "plane", "own"]
-    peer = cores[rank["peer", False]]
-    off = topo.mask(core, cores[rank["far", True]])
-    inner = topo.mask(core, peer) & ~off
+    off = topo.mask(core, cores[rank[FAR]])
+    whole = topo.mask(core, cores[rank[PEER]])
+    inner = whole & ~off
+    half0, half1 = _split(off, 2)
+    slot = {p: i for i, p in enumerate(SLOTS)}
     sem = T.sem
     cnt = lambda m: len(_engines(m))
 
@@ -88,8 +95,16 @@ def rank_program(g, core, T, topo):
             ids.append(DstId(rid=rid, pnc=pid))
         return RemoteDMATransfer(dst_ids=ids, dma_engine_mask=mask, remote_sem=rsem, srcs=[src], dsts=[v for _, v in dests])
 
-    for i, k in enumerate(order):
-        lo, hi = E * chip_of[k][0], E * (chip_of[k][-1] + 1)
+    def there(buf, p):
+        return cores[rank[p]], tile(buf, slot[p])
+
+    def there8(p):
+        c, v = there(T.hl, p)
+        return c, bytes_(v)
+
+    spans = [sorted(rank[p] for p in ps) for ps in LOADS]
+    for i, rs in enumerate(spans):
+        lo, hi = E * rs[0], E * (rs[-1] + 1)
         g.sync.dma_start(T.bt[0:64, lo:hi], T.b[0:64, lo:hi]).then_inc(sem["bload%d" % i], 16)
         g.scalar.dma_start(T.bt[64:128, lo:hi], T.b[64:128, lo:hi]).then_inc(sem["bload%d" % i], 16)
 
@@ -97,43 +112,48 @@ def rank_program(g, core, T, topo):
     g.vector.memset(T.diag[:], 0.0).then_inc(sem.fill, 1)
     g.wait_ge(sem.fill, 2)
     g.affine_select(T.diag[:, 3:3 + E:4], T.ones[:], [[1, W]], AluOpType.is_equal, 0.0, 0, -1).then_inc(sem.dia, 1)
-    g.vector.wait_ge(sem.dia, 1)
-    for b in range(4):
-        g.vector.quantize_mx(tile(T.sq, b), tile(T.ss, b), T.diag[:, 3 - b:3 - b + E]).then_inc(sem.sdone, 1)
 
-    for i, k in enumerate(order):
-        r0, n = chip_of[k][0], len(chip_of[k])
+    for i, rs in enumerate(spans):
+        if i == 2:
+            g.vector.wait_ge(sem.dia, 1)
+            for b in range(4):
+                g.vector.quantize_mx(tile(T.sq, b), tile(T.ss, b), T.diag[:, 3 - b:3 - b + E]).then_inc(sem.sdone, 1)
+        r0, n = rs[0], len(rs)
         g.vector.wait_ge(sem["bload%d" % i], 32)
         g.vector.quantize_mx(tile(T.q, r0, n), tile(T.qs, r0, n),
                              T.bt[:, E * r0:E * (r0 + n)]).then_inc(sem["bdone%d" % i], 1)
 
-    def scatter(plan):
-        mine = sem["from%d" % me]
-        g.remote_dma_fused([send(m, mine, bytes_(tile(T.q, r)), [(cores[r], bytes_(tile(T.land, me)))])
-                            for r, m in plan], local_sem=sem.sent1)
-        g.remote_dma_fused([send(m, mine, tile(T.qs, r), [(cores[r], tile(T.lands, me))])
-                            for r, m in plan], local_sem=sem.sent1)
-        return 2 * sum(cnt(m) for _, m in plan)
-
-    plan1 = list(zip(chip_of["far"], _split(off, 2)))
-    plan2 = list(zip(chip_of["mate"] + chip_of["plane"], _split(off, 4))) + [(rank["peer", False], inner)]
-    g.wait_ge(sem.bdone0, 1)
-    out1 = scatter(plan1)
-    for i in (1, 2, 3):
-        g.wait_ge(sem["bdone%d" % i], 1)
-    out1 += scatter(plan2)
+    arrival = sem["from%d" % me]
+    out1 = [0]
     came = {}
-    for r, m in plan1 + plan2:
-        came[r] = 2 * cnt(m)
+
+    def scatter(plan):
+        g.remote_dma_fused([send(m, arrival, bytes_(tile(T.q, rank[p])), [(cores[rank[p]], bytes_(tile(T.land, me)))])
+                            for p, m in plan], local_sem=sem.sent1)
+        g.remote_dma_fused([send(m, arrival, tile(T.qs, rank[p]), [(cores[rank[p]], tile(T.lands, me))])
+                            for p, m in plan], local_sem=sem.sent1)
+        for p, m in plan:
+            came[p] = 2 * cnt(m)
+            out1[0] += 2 * cnt(m)
+
+    g.wait_ge(sem.bdone0, 1)
+    scatter([(PLANE, off)])
+    g.wait_ge(sem.bdone1, 1)
+    scatter([(FAR, half0), (FAR_X, half1)])
+    for i in (2, 3, 4):
+        g.wait_ge(sem["bdone%d" % i], 1)
+    scatter([(MATE, half0), (PLANE_X, half1), (PEER, inner)])
+    scatter([(MATE_X, off)])
 
     g.tensor.wait_ge(sem.sdone, 4)
-    g.tensor.wait_ge(sem.bdone3, 1)
-    sources = [me] + [rank[p] for p in (("far", True), ("far", False), ("peer", False), ("mate", True), ("mate", False),
-                                        ("plane", True), ("plane", False))]
-    for i, r in enumerate(sources):
-        cod, sca = (T.q, T.qs) if r == me else (T.land, T.lands)
-        if r != me:
-            g.tensor.wait_ge(sem["from%d" % r], came[r])
+    for i, p in enumerate(SUMS):
+        r = rank[p]
+        if p == OWN:
+            g.tensor.wait_ge(sem.bdone4, 1)
+            cod, sca = T.q, T.qs
+        else:
+            g.tensor.wait_ge(sem["from%d" % r], came[p])
+            cod, sca = T.land, T.lands
         for b in range(4):
             mm = g.tensor.matmul_mx(T.ps[:, BANK * b:BANK * b + W], tile(T.sq, b), tile(T.ss, b),
                                     tile(cod, r), tile(sca, r), i == 0, i == N - 1)
@@ -151,65 +171,57 @@ def rank_program(g, core, T, topo):
     g.vector.wait_ge(sem.hop, 4)
     g.vector.quantize_mx(T.hq[:], T.hs[:], T.ht[:]).then_inc(sem.hdone, 1)
 
-    g.sync.wait_ge(sem.sent1, out1)
+    g.sync.wait_ge(sem.sent1, out1[0])
     g.sync.dma_start(T.xt[:], T.x[:]).then_inc(sem.xload, 16)
     g.vector.wait_ge(sem.xload, 16)
     g.vector.quantize_mx(T.xq[:], T.xs[:], T.xt[:]).then_inc(sem.xdone, 1)
 
-    slot = {p: i for i, p in enumerate(SLOTS)}
-
-    def there(buf, p):
-        return cores[rank[p]], tile(buf, slot[p])
-
-    def there8(p):
-        c, v = there(T.hl, p)
-        return c, bytes_(v)
-
-    first = [("plane", True), ("far", True)]
-    near = ("peer", False)
-    mate = [("mate", True), ("mate", False)]
     g.wait_ge(sem.hdone, 1)
-    g.remote_dma_fused([send(off, sem.hcod, bytes_(T.hq[:]), [there8(p) for p in first]),
-                        send(inner, sem.hpeer, bytes_(T.hq[:]), [there8(near)])], local_sem=sem.sent2)
-    g.remote_dma_fused([send(off, sem.hsca, T.hs[:], [there(T.hls, p) for p in first]),
-                        send(inner, sem.hpeer, T.hs[:], [there(T.hls, near)])], local_sem=sem.sent2)
-    g.remote_dma_fused([send(off, sem.hmate, bytes_(T.hq[:]), [there8(p) for p in mate])], local_sem=sem.sent2)
-    g.remote_dma_fused([send(off, sem.hmate, T.hs[:], [there(T.hls, p) for p in mate])], local_sem=sem.sent2)
-    out2 = 4 * cnt(off) + 2 * cnt(inner)
-    rid, pid = topo.addr(peer, core)
-    s0, o0 = slot["plane", True], slot["plane", False]
-    g.wait_ge(sem.hcod, 2 * cnt(off))
-    g.remote_dma(bytes_(tile(T.hl, o0, 2)), bytes_(tile(T.hl, s0, 2)), sem.hfwd, sem.sent3, pid, rid, inner)
+    hq8 = bytes_(T.hq[:])
+    g.remote_dma_fused([send(off, sem.hfar, hq8, [there8(FAR)]), send(inner, sem.hpeer, hq8, [there8(PEER)])], local_sem=sem.sent2)
+    g.remote_dma_fused([send(off, sem.hplane, hq8, [there8(PLANE)])], local_sem=sem.sent2)
+    g.remote_dma_fused([send(off, sem.hsca, T.hs[:], [there(T.hls, PLANE), there(T.hls, FAR)]),
+                        send(inner, sem.hpeer, T.hs[:], [there(T.hls, PEER)])], local_sem=sem.sent2)
+    pair = ((half0, sem.hmate, MATE), (half1, sem.hmatex, MATE_X))
+    g.remote_dma_fused([send(m, s, hq8, [there8(p)]) for m, s, p in pair], local_sem=sem.sent2)
+    g.remote_dma_fused([send(m, s, T.hs[:], [there(T.hls, p)]) for m, s, p in pair], local_sem=sem.sent2)
+    out2 = 5 * cnt(off) + 2 * cnt(inner)
+    rid, pid = topo.addr(cores[rank[PEER]], core)
+    g.wait_ge(sem.hfar, cnt(off))
+    g.remote_dma(bytes_(tile(T.hl, slot[FAR_X])), bytes_(tile(T.hl, slot[FAR])), sem.hfwd, sem.sent3, pid, rid, inner)
+    g.wait_ge(sem.hplane, cnt(off))
+    g.remote_dma(bytes_(tile(T.hl, slot[PLANE_X])), bytes_(tile(T.hl, slot[PLANE])), sem.hfwd, sem.sent3, pid, rid, whole)
     g.wait_ge(sem.hsca, 2 * cnt(off))
-    g.remote_dma(tile(T.hls, o0, 2), tile(T.hls, s0, 2), sem.hfwd, sem.sent3, pid, rid, inner)
-    g.wait_ge(sem.sent3, 2 * cnt(inner))
+    g.remote_dma(tile(T.hls, slot[PLANE_X], 2), tile(T.hls, slot[PLANE], 2), sem.hfwd, sem.sent3, pid, rid, whole)
+    passed = cnt(inner) + 2 * cnt(whole)
+    g.wait_ge(sem.sent3, passed)
 
-    arrive = {"own": [], "peer": [("hpeer", 2 * cnt(inner))], "mate": [("hmate", 4 * cnt(off))],
-              True: [("hcod", 2 * cnt(off)), ("hsca", 2 * cnt(off))], False: [("hfwd", 2 * cnt(inner))]}
-    blocks = [("own", True), near, ("plane", True), ("far", True), ("mate", True), ("mate", False),
-              ("plane", False), ("far", False)]
+    scales, handed = (sem.hsca, 2 * cnt(off)), (sem.hfwd, passed)
+    arrive = {PEER: [(sem.hpeer, 2 * cnt(inner))], PLANE: [(sem.hplane, cnt(off)), scales], FAR: [(sem.hfar, cnt(off)), scales],
+              MATE: [(sem.hmate, 2 * cnt(half0))], MATE_X: [(sem.hmatex, 2 * cnt(half1))], PLANE_X: [handed], FAR_X: [handed]}
     g.tensor.wait_ge(sem.hdone, 1)
     g.tensor.wait_ge(sem.xdone, 1)
-    for i, p in enumerate(blocks):
+    for i, p in enumerate(BLOCKS):
         j = rank[p]
         bank = BANK * ((i + 4) % 8)
-        if p[0] == "own":
+        if p == OWN:
             w, ws = T.hq[:], T.hs[:]
         else:
-            for s, v in arrive[p[0] if p[0] in arrive else p[1]]:
-                g.tensor.wait_ge(sem[s], v)
+            for s, v in arrive[p]:
+                g.tensor.wait_ge(s, v)
             w, ws = tile(T.hl, slot[p]), tile(T.hls, slot[p])
         g.tensor.matmul_mx(T.ps[:, bank:bank + W], w, ws, T.xq[:], T.xs[:], True, True).then_inc(sem["yps%d" % j], 1)
     stores = [0]
 
-    def store(queue, js):
+    def store(queue, ps):
+        js = sorted(rank[p] for p in ps)
         for j in js:
             queue.wait_ge(sem["ysb%d" % j], 1)
         lo, hi = W * js[0], W * (js[-1] + 1)
         queue.dma_start(T.y[:, lo:hi], T.yt[:, lo:hi]).then_inc(sem.stored, 16)
         stores[0] += 1
 
-    for i, p in enumerate(blocks):
+    for i, p in enumerate(BLOCKS):
         j = rank[p]
         bank = BANK * ((i + 4) % 8)
         if i % 2 == 0:
@@ -219,15 +231,15 @@ def rank_program(g, core, T, topo):
             g.scalar.wait_ge(sem["yps%d" % j], 1)
             g.scalar.activation(tile(T.yt, j), T.ps[:, bank:bank + W],
                                 ActivationFunctionType.Copy).then_inc(sem["ysb%d" % j], 1)
-        if p == ("mate", False):
-            store(g.scalar, chip_of["mate"])
-    store(g.scalar, [rank["far", False]])
+        if p == MATE_X:
+            store(g.scalar, [MATE, MATE_X])
+    store(g.scalar, [FAR_X])
 
     g.sync.wait_ge(sem.sent2, out2)
-    store(g.sync, chip_of["own"])
-    store(g.sync, [rank["plane", True]])
-    store(g.sync, [rank["far", True]])
+    store(g.sync, [OWN, PEER])
+    store(g.sync, [PLANE])
+    store(g.sync, [FAR])
     g.sync.wait_ge(sem.hop, 4)
     g.sync.dma_start(T.h[:], T.ht[:]).then_inc(sem.stored, 16)
-    store(g.sync, [rank["plane", False]])
+    store(g.sync, [PLANE_X])
     g.sync.wait_ge(sem.stored, 16 * (stores[0] + 1))

import numpy as np
from concourse.bass import DstId, RemoteDMATransfer
from concourse.mybir import dt, AluOpType, ActivationFunctionType

N = 8
W = 128
E = 4 * W
BANK = 512
C2 = float(np.float32(0.344))

OWN, PEER = ("own", True), ("peer", False)
MATE, MATE_X = ("mate", True), ("mate", False)
PLANE, PLANE_X = ("plane", True), ("plane", False)
FAR, FAR_X = ("far", True), ("far", False)

LOADS = [[PLANE], [FAR, FAR_X], [PLANE_X], [MATE, MATE_X], [OWN, PEER]]
SUMS = [OWN, PLANE, FAR, FAR_X, PEER, MATE, PLANE_X, MATE_X]
SLOTS = [PLANE, FAR, PLANE_X, FAR_X, MATE, MATE_X, PEER]
BLOCKS = [OWN, PEER, PLANE, FAR, MATE, MATE_X, PLANE_X, FAR_X]

SCRATCH = {
    "bt": ("sbuf", [128, N * E], "bfloat16"),
    "q": ("sbuf", [128, N * W], "float8_e4m3fn_x4"),
    "qs": ("sbuf", [128, N * W], "uint8"),
    "land": ("sbuf", [128, N * W], "float8_e4m3fn_x4"),
    "lands": ("sbuf", [128, N * W], "uint8"),
    "xt": ("sbuf", [128, E], "bfloat16"),
    "xq": ("sbuf", [128, W], "float8_e4m3fn_x4"),
    "xs": ("sbuf", [128, W], "uint8"),
    "ones": ("sbuf", [128, W], "bfloat16"),
    "diag": ("sbuf", [128, E + 4], "bfloat16"),
    "sq": ("sbuf", [128, 4 * W], "float8_e4m3fn_x4"),
    "ss": ("sbuf", [128, 4 * W], "uint8"),
    "ht": ("sbuf", [128, E], "bfloat16"),
    "hq": ("sbuf", [128, W], "float8_e4m3fn_x4"),
    "hs": ("sbuf", [128, W], "uint8"),
    "hl": ("sbuf", [128, 7 * W], "float8_e4m3fn_x4"),
    "hls": ("sbuf", [128, 7 * W], "uint8"),
    "yt": ("sbuf", [128, N * W], "float32"),
    "ps": ("psum", [128, 8 * BANK], "float32"),
}
SEMAPHORES = (["fill", "dia", "sdone", "xload", "xdone", "hop", "hdone", "sent1", "sent2", "sent3", "stored",
               "hpeer", "hplane", "hfar", "hmate", "hmatex", "hsca", "hfwd"]
              + ["bload%d" % i for i in range(len(LOADS))] + ["bdone%d" % i for i in range(len(LOADS))]
              + ["from%d" % i for i in range(N)] + ["z%d" % i for i in range(4)]
              + ["yps%d" % i for i in range(N)] + ["ysb%d" % i for i in range(N)])


def _engines(mask):
    return [i for i in range(mask.bit_length()) if mask >> i & 1]


def _split(mask, k):
    e = _engines(mask)
    n = len(e) // k
    return [sum(1 << i for i in e[j * n:j * n + n]) for j in range(k)]


def _place(topo, a, b):
    if (topo.host(a), topo.chip(a)) == (topo.host(b), topo.chip(b)):
        kind = "own" if a == b else "peer"
    elif topo.mates(a, b):
        kind = "mate"
    elif topo.same_plane(a, b):
        kind = "plane"
    else:
        kind = "far"
    return kind, topo.die(a) == topo.die(b)


def rank_program(g, core, T, topo):
    cores = list(T.cores)
    me = T.rank_of(core)
    if me is None:
        return
    rank = {_place(topo, core, c): r for r, c in enumerate(cores)}
    off = topo.mask(core, cores[rank[FAR]])
    whole = topo.mask(core, cores[rank[PEER]])
    inner = whole & ~off
    half0, half1 = _split(off, 2)
    slot = {p: i for i, p in enumerate(SLOTS)}
    sem = T.sem
    cnt = lambda m: len(_engines(m))

    def tile(buf, i, n=1):
        return buf[:, W * i:W * (i + n)]

    def bytes_(ap):
        return ap.bitcast(dt.uint8)

    def send(mask, rsem, src, dests):
        ids = []
        for c, _ in dests:
            rid, pid = topo.addr(c, core)
            ids.append(DstId(rid=rid, pnc=pid))
        return RemoteDMATransfer(dst_ids=ids, dma_engine_mask=mask, remote_sem=rsem, srcs=[src], dsts=[v for _, v in dests])

    def there(buf, p):
        return cores[rank[p]], tile(buf, slot[p])

    def there8(p):
        c, v = there(T.hl, p)
        return c, bytes_(v)

    spans = [sorted(rank[p] for p in ps) for ps in LOADS]
    for i, rs in enumerate(spans):
        lo, hi = E * rs[0], E * (rs[-1] + 1)
        g.sync.dma_start(T.bt[0:64, lo:hi], T.b[0:64, lo:hi]).then_inc(sem["bload%d" % i], 16)
        g.scalar.dma_start(T.bt[64:128, lo:hi], T.b[64:128, lo:hi]).then_inc(sem["bload%d" % i], 16)

    g.vector.memset(T.ones[:], 1.0).then_inc(sem.fill, 1)
    g.vector.memset(T.diag[:], 0.0).then_inc(sem.fill, 1)
    g.wait_ge(sem.fill, 2)
    g.affine_select(T.diag[:, 3:3 + E:4], T.ones[:], [[1, W]], AluOpType.is_equal, 0.0, 0, -1).then_inc(sem.dia, 1)

    for i, rs in enumerate(spans):
        if i == 2:
            g.vector.wait_ge(sem.dia, 1)
            for b in range(4):
                g.vector.quantize_mx(tile(T.sq, b), tile(T.ss, b), T.diag[:, 3 - b:3 - b + E]).then_inc(sem.sdone, 1)
        r0, n = rs[0], len(rs)
        g.vector.wait_ge(sem["bload%d" % i], 32)
        g.vector.quantize_mx(tile(T.q, r0, n), tile(T.qs, r0, n),
                             T.bt[:, E * r0:E * (r0 + n)]).then_inc(sem["bdone%d" % i], 1)

    arrival = sem["from%d" % me]
    out1 = [0]
    came = {}

    def scatter(plan):
        g.remote_dma_fused([send(m, arrival, bytes_(tile(T.q, rank[p])), [(cores[rank[p]], bytes_(tile(T.land, me)))])
                            for p, m in plan], local_sem=sem.sent1)
        g.remote_dma_fused([send(m, arrival, tile(T.qs, rank[p]), [(cores[rank[p]], tile(T.lands, me))])
                            for p, m in plan], local_sem=sem.sent1)
        for p, m in plan:
            came[p] = 2 * cnt(m)
            out1[0] += 2 * cnt(m)

    g.wait_ge(sem.bdone0, 1)
    scatter([(PLANE, off)])
    g.wait_ge(sem.bdone1, 1)
    scatter([(FAR, half0), (FAR_X, half1)])
    for i in (2, 3, 4):
        g.wait_ge(sem["bdone%d" % i], 1)
    scatter([(MATE, half0), (PLANE_X, half1), (PEER, inner)])
    scatter([(MATE_X, off)])

    g.tensor.wait_ge(sem.sdone, 4)
    for i, p in enumerate(SUMS):
        r = rank[p]
        if p == OWN:
            g.tensor.wait_ge(sem.bdone4, 1)
            cod, sca = T.q, T.qs
        else:
            g.tensor.wait_ge(sem["from%d" % r], came[p])
            cod, sca = T.land, T.lands
        for b in range(4):
            mm = g.tensor.matmul_mx(T.ps[:, BANK * b:BANK * b + W], tile(T.sq, b), tile(T.ss, b),
                                    tile(cod, r), tile(sca, r), i == 0, i == N - 1)
            if i == N - 1:
                mm.then_inc(sem["z%d" % b], 1)

    for b in (0, 2):
        g.scalar.wait_ge(sem["z%d" % b], 1)
        g.scalar.activation(T.ht[:, b:E:4], T.ps[:, BANK * b:BANK * b + W], ActivationFunctionType.Relu,
                            scale=C2).then_inc(sem.hop, 1)
    for b in (1, 3):
        g.vector.wait_ge(sem["z%d" % b], 1)
        g.vector.tensor_scalar(T.ht[:, b:E:4], T.ps[:, BANK * b:BANK * b + W], 0.0, C2,
                               AluOpType.max, AluOpType.mult).then_inc(sem.hop, 1)
    g.vector.wait_ge(sem.hop, 4)
    g.vector.quantize_mx(T.hq[:], T.hs[:], T.ht[:]).then_inc(sem.hdone, 1)

    g.sync.wait_ge(sem.sent1, out1[0])
    g.sync.dma_start(T.xt[:], T.x[:]).then_inc(sem.xload, 16)
    g.vector.wait_ge(sem.xload, 16)
    g.vector.quantize_mx(T.xq[:], T.xs[:], T.xt[:]).then_inc(sem.xdone, 1)

    g.wait_ge(sem.hdone, 1)
    hq8 = bytes_(T.hq[:])
    g.remote_dma_fused([send(off, sem.hfar, hq8, [there8(FAR)]), send(inner, sem.hpeer, hq8, [there8(PEER)])], local_sem=sem.sent2)
    g.remote_dma_fused([send(off, sem.hplane, hq8, [there8(PLANE)])], local_sem=sem.sent2)
    g.remote_dma_fused([send(off, sem.hsca, T.hs[:], [there(T.hls, PLANE), there(T.hls, FAR)]),
                        send(inner, sem.hpeer, T.hs[:], [there(T.hls, PEER)])], local_sem=sem.sent2)
    pair = ((half0, sem.hmate, MATE), (half1, sem.hmatex, MATE_X))
    g.remote_dma_fused([send(m, s, hq8, [there8(p)]) for m, s, p in pair], local_sem=sem.sent2)
    g.remote_dma_fused([send(m, s, T.hs[:], [there(T.hls, p)]) for m, s, p in pair], local_sem=sem.sent2)
    out2 = 5 * cnt(off) + 2 * cnt(inner)
    rid, pid = topo.addr(cores[rank[PEER]], core)
    g.wait_ge(sem.hfar, cnt(off))
    g.remote_dma(bytes_(tile(T.hl, slot[FAR_X])), bytes_(tile(T.hl, slot[FAR])), sem.hfwd, sem.sent3, pid, rid, inner)
    g.wait_ge(sem.hplane, cnt(off))
    g.remote_dma(bytes_(tile(T.hl, slot[PLANE_X])), bytes_(tile(T.hl, slot[PLANE])), sem.hfwd, sem.sent3, pid, rid, whole)
    g.wait_ge(sem.hsca, 2 * cnt(off))
    g.remote_dma(tile(T.hls, slot[PLANE_X], 2), tile(T.hls, slot[PLANE], 2), sem.hfwd, sem.sent3, pid, rid, whole)
    passed = cnt(inner) + 2 * cnt(whole)
    g.wait_ge(sem.sent3, passed)

    scales, handed = (sem.hsca, 2 * cnt(off)), (sem.hfwd, passed)
    arrive = {PEER: [(sem.hpeer, 2 * cnt(inner))], PLANE: [(sem.hplane, cnt(off)), scales], FAR: [(sem.hfar, cnt(off)), scales],
              MATE: [(sem.hmate, 2 * cnt(half0))], MATE_X: [(sem.hmatex, 2 * cnt(half1))], PLANE_X: [handed], FAR_X: [handed]}
    g.tensor.wait_ge(sem.hdone, 1)
    g.tensor.wait_ge(sem.xdone, 1)
    for i, p in enumerate(BLOCKS):
        j = rank[p]
        bank = BANK * ((i + 4) % 8)
        if p == OWN:
            w, ws = T.hq[:], T.hs[:]
        else:
            for s, v in arrive[p]:
                g.tensor.wait_ge(s, v)
            w, ws = tile(T.hl, slot[p]), tile(T.hls, slot[p])
        g.tensor.matmul_mx(T.ps[:, bank:bank + W], w, ws, T.xq[:], T.xs[:], True, True).then_inc(sem["yps%d" % j], 1)
    stores = [0]

    def store(queue, ps):
        js = sorted(rank[p] for p in ps)
        for j in js:
            queue.wait_ge(sem["ysb%d" % j], 1)
        lo, hi = W * js[0], W * (js[-1] + 1)
        queue.dma_start(T.y[:, lo:hi], T.yt[:, lo:hi]).then_inc(sem.stored, 16)
        stores[0] += 1

    for i, p in enumerate(BLOCKS):
        j = rank[p]
        bank = BANK * ((i + 4) % 8)
        if i % 2 == 0:
            g.vector.wait_ge(sem["yps%d" % j], 1)
            g.vector.tensor_copy(tile(T.yt, j), T.ps[:, bank:bank + W]).then_inc(sem["ysb%d" % j], 1)
        else:
            g.scalar.wait_ge(sem["yps%d" % j], 1)
            g.scalar.activation(tile(T.yt, j), T.ps[:, bank:bank + W],
                                ActivationFunctionType.Copy).then_inc(sem["ysb%d" % j], 1)
        if p == MATE_X:
            store(g.scalar, [MATE, MATE_X])
    store(g.scalar, [FAR_X])

    g.sync.wait_ge(sem.sent2, out2)
    store(g.sync, [OWN, PEER])
    store(g.sync, [PLANE])
    store(g.sync, [FAR])
    g.sync.wait_ge(sem.hop, 4)
    g.sync.dma_start(T.h[:], T.ht[:]).then_inc(sem.stored, 16)
    store(g.sync, [PLANE_X])
    g.sync.wait_ge(sem.stored, 16 * (stores[0] + 1))
